import numpy as np
import ml_dtypes


def mxq(x, axis, fmt="e4m3"):
    dtype, down = {"e4m3": (ml_dtypes.float8_e4m3fn, 7), "e5m2": (ml_dtypes.float8_e5m2, 14)}[fmt]
    v = np.moveaxis(np.asarray(x, np.float32).astype(ml_dtypes.bfloat16).astype(np.float64), axis, -1)
    blocks = v.reshape(v.shape[:-1] + (-1, 32))
    amax = np.abs(blocks).max(-1, keepdims=True)
    byte = np.maximum(np.where(amax > 0, np.frexp(amax)[1] - 1 + 127, 0) - down, 1)
    scale = np.exp2(byte - 127.0)
    codes = (blocks / scale).astype(np.float32).astype(dtype).astype(np.float64)
    return np.moveaxis((codes * scale).reshape(v.shape), -1, axis)


WIDE = False


def mx_kscale(k):
    if not WIDE:
        return np.ones(k)
    levels = np.array([30, -30])
    if k % 512:
        return np.exp2(np.random.permutation(np.resize(levels, k // 32))).repeat(32)
    a = np.empty((k // 512, 16))
    for p in range(k // 512):
        a[p, :8] = np.random.permutation(np.resize(levels, 8))
        for g in range(8):
            far = levels[np.abs(levels - a[p, g]) >= 10]
            a[p, g + 8] = far[np.random.randint(len(far))]
    return np.exp2(a.ravel()).repeat(32)


def f64(x):
    return np.asarray(x).astype(np.float64)


def striped(idx):
    return np.tile(np.asarray(idx).reshape(-1, 16).T, (8, 1)).astype(np.uint16)


def unstriped(offs):
    return offs[:16].T.reshape(-1).astype(np.int64)


E2M1 = np.array([0.0, 0.5, 1.0, 1.5, 2.0, 3.0, 4.0, 6.0, -0.0, -0.5, -1.0, -1.5, -2.0, -3.0, -4.0, -6.0])


def pack_weight(w, fmt):
    k, n = w.shape
    w = f64(np.asarray(w, np.float32).astype(ml_dtypes.bfloat16)).reshape(k // 32, 32, n)
    amax = np.abs(w).max(1)
    if fmt in ("e4m3", "e5m2"):
        byte = np.frexp(amax)[1] - 1 + 127 - (7 if fmt == "e4m3" else 14)
    else:
        mant, ex = np.frexp(amax / 6.0)
        byte = np.where(mant > 0.5, ex, ex - 1) + 127
    byte = np.clip(np.where(amax > 0, byte, 1), 1, 254)
    scaled = (w * np.exp2(127.0 - byte)[:, None, :]).reshape(k, n).astype(np.float32)
    by_word = np.ascontiguousarray(scaled.reshape(k // 512, 128, 4, n).transpose(0, 1, 3, 2))
    if fmt in ("e4m3", "e5m2"):
        words = by_word.astype(ml_dtypes.float8_e4m3fn if fmt == "e4m3" else ml_dtypes.float8_e5m2).view(np.uint8)
    else:
        c = by_word.astype(ml_dtypes.float4_e2m1fn).view(np.uint8) & 0xF
        words = (c[..., 0::2] | (c[..., 1::2] << 4)).reshape(k // 512, 128, 2 * n)
    return np.ascontiguousarray(words), np.ascontiguousarray(byte.astype(np.uint8).reshape(k // 512, 16, n))


def unpack_weight(words, scales, fmt):
    g, _, n = scales.shape
    words = np.ascontiguousarray(words).reshape(g, 128, n, -1)
    if fmt in ("e4m3", "e5m2"):
        vals = words.view(ml_dtypes.float8_e4m3fn if fmt == "e4m3" else ml_dtypes.float8_e5m2).astype(np.float64)
    else:
        nib = np.empty((g, 128, n, 4), np.uint8)
        nib[..., 0::2] = words & 0xF
        nib[..., 1::2] = words >> 4
        vals = E2M1[nib]
    vals = vals * np.repeat(np.exp2(scales.astype(np.float64) - 127.0), 8, axis=1)[..., None]
    return vals.transpose(0, 1, 3, 2).reshape(g * 512, n)


def bf(x):
    return np.asarray(x, np.float32).astype(ml_dtypes.bfloat16)


def planes(Y):
    r, m = Y.shape
    b = f64(bf(Y)).reshape(r // 32, 32, m)
    amax = np.abs(b).max(1)
    byte = np.clip(np.where(amax > 0, np.frexp(amax)[1] - 1 + 127 - 7, 1), 1, 254)
    codes = (b * np.exp2(127.0 - byte)[:, None, :]).reshape(r, m).astype(np.float32).astype(ml_dtypes.float8_e4m3fn).view(np.uint8)
    words = codes.reshape(r // 512, 128, 4, m).transpose(0, 1, 3, 2)
    return np.ascontiguousarray(words), np.ascontiguousarray(byte.astype(np.uint8).reshape(r // 512, 16, m))


K, T, J, B, R, V, N, Z = 1024, 1024, 384, 48, 512, 512, 512, 512


def setup_inputs():
    n = np.random.standard_normal
    idx = np.random.permutation(T)[:J]
    idx2 = np.random.permutation(V)[:J]
    idx3 = np.random.permutation(Z)[:J]
    fk = mx_kscale(K)
    fr = mx_kscale(R)
    wp = pack_weight(n((K, R)) * 1 / np.sqrt(K) * fk[:, None] * fr, "e5m2")
    wbp = pack_weight(n((R, N)) * 1 / np.sqrt(R) / fr[:, None], "e5m2")
    return {
        "xf": (n((K, T))).astype(np.float32),
        "fk": (np.random.uniform(0.5, 2.0, (K, 1)) / fk[:, None]).astype(np.float32),
        "w_words": wp[0],
        "w_scales": wp[1],
        "tb": (n((R, V)) * 0.7).astype(np.float32),
        "wb_words": wbp[0],
        "wb_scales": wbp[1],
        "tz": (n((N, Z))).astype(np.float32),
        "offs": striped(idx),
        "offs2": striped(idx2),
        "offs3": striped(idx3),
    }


def reference(xf, fk, w_words, w_scales, tb, wb_words, wb_scales, tz, offs, offs2, offs3):
    idx = unstriped(offs)
    idx2 = unstriped(offs2)
    idx3 = unstriped(offs3)
    wu = unpack_weight(w_words, w_scales, "e5m2")
    wbu = unpack_weight(wb_words, wb_scales, "e5m2")
    xg = f64(xf)[:, idx]
    g1 = xg.reshape(K, B, J // B).mean(axis=2)
    g2 = np.repeat(g1, J // B, axis=1)
    u = (xg - g2) * f64(fk)
    uq = mxq(u, 0, "e4m3")
    a = wu.T @ uq
    hid = np.maximum(a, 0.0) * f64(tb)[:, idx2]
    hidq = mxq(hid, 0, "e4m3")
    p = wbu.T @ hidq
    y = p * f64(tz)[:, idx3]
    words, scales = planes(y)
    return y, words, scales

@@ -1,0 +1,249 @@
+from contextlib import ExitStack
+
+import concourse.mybir as mybir
+
+K, T, J, R, V, N, Z = 1024, 1024, 384, 512, 512, 512, 512
+GROUP = 8
+B = J // GROUP
+FLOPS = 2 * K * R * J + 2 * R * N * J
+
+F32 = mybir.dt.float32
+BF16 = mybir.dt.bfloat16
+I32 = mybir.dt.int32
+U32 = mybir.dt.uint32
+U16 = mybir.dt.uint16
+U8 = mybir.dt.uint8
+E4M3X4 = mybir.dt.float8_e4m3fn_x4
+E5M2X4 = mybir.dt.float8_e5m2_x4
+ALU = mybir.AluOpType
+COPY = mybir.ActivationFunctionType.Copy
+AX = mybir.AxisListType
+
+P = 128
+PACK = 4
+PASSES = K // (P * PACK)
+CHUNK = 128
+CHUNKS = J // CHUNK
+
+
+def tile_list_centredpicks_timestable_timeslook_pl_kernel(
+    tc, xf, fk, w_words, w_scales, tb, wb_words, wb_scales, tz, offs, offs2, offs3, out_0, out_1, out_2
+):
+    nc = tc.nc
+    with ExitStack() as ctx:
+        keep = ctx.enter_context(tc.tile_pool(name="keep", bufs=1))
+        psum = ctx.enter_context(tc.psum_pool(name="psum", bufs=1))
+
+        lists = [keep.tile([P, J // 16], U16, name="list%d" % i) for i in range(3)]
+        fk_sb = keep.tile([P, PASSES, PACK], F32, name="fk_sb")
+        x_win = [keep.tile([P, T], F32, name="x_win%d" % i) for i in range(PASSES * PACK)]
+        tb_win = [keep.tile([P, V], F32, name="tb_win%d" % t) for t in range(PACK)]
+        tz_win = [keep.tile([P, Z], F32, name="tz_win%d" % t) for t in range(PACK)]
+        w_raw = [keep.tile([P, R], U32, name="w_raw%d" % a) for a in range(PASSES)]
+        wb_raw = keep.tile([P, N], U32, name="wb_raw")
+        ws_raw = keep.tile([P, PASSES, R], U8, name="ws_raw")
+        wbs_raw = keep.tile([P, N], U8, name="wbs_raw")
+        w_codes = [keep.tile([P, PACK, P], U32, name="w_codes%d" % a, align_bytes=64) for a in range(PASSES)]
+        wb_codes = keep.tile([P, PACK, P], U32, name="wb_codes", align_bytes=64)
+        w_sc = keep.tile([P, PASSES, PACK, P], U8, name="w_sc", align_bytes=64)
+        wb_sc = keep.tile([P, PACK, P], U8, name="wb_sc", align_bytes=64)
+
+        nc.gpsimd.memset(ws_raw[:].rearrange("p a c -> p (a c)").bitcast(I32), 0)
+        nc.gpsimd.memset(wbs_raw[:].bitcast(I32), 0)
+
+        x_rows = xf.rearrange("(a p t) c -> a t p c", a=PASSES, t=PACK)
+        tb_rows = tb.rearrange("(p t) c -> t p c", t=PACK)
+        tz_rows = tz.rearrange("(p t) c -> t p c", t=PACK)
+
+        def load_w_scales(q):
+            nc.sync.dma_start(
+                out=ws_raw[32 * q : 32 * q + 4].bitcast(I32),
+                in_=w_scales[:, 4 * q : 4 * q + 4, :].rearrange("a r c -> r a c").bitcast(I32),
+            )
+
+        def load_wb_scales(q):
+            nc.sync.dma_start(
+                out=wbs_raw[32 * q : 32 * q + 4].bitcast(I32), in_=wb_scales[0, 4 * q : 4 * q + 4, :].bitcast(I32)
+            )
+
+        def load_x(i):
+            nc.sync.dma_start(out=x_win[i][:], in_=x_rows[i // PACK, i % PACK])
+
+        nc.scalar.dma_start(out=fk_sb[:], in_=fk.rearrange("(a p t) o -> p a (t o)", a=PASSES, t=PACK))
+        nc.sync.dma_start(lists[0][:], offs)
+        load_x(0)
+        load_x(1)
+        for q in (0, 2):
+            load_w_scales(q)
+            load_w_scales(q + 1)
+            load_x(2 + q // 2)
+        for q in (0, 2):
+            load_wb_scales(q)
+            load_wb_scales(q + 1)
+            load_x(4 + q // 2)
+        load_x(6)
+        nc.sync.dma_start(lists[1][:], offs2)
+        load_x(7)
+        for t in range(PACK):
+            nc.sync.dma_start(out=tb_win[t][:], in_=tb_rows[t])
+            if t < PASSES:
+                nc.sync.dma_start(
+                    out=w_raw[t][:].bitcast(I32), in_=w_words[t].rearrange("p c t -> p (c t)").bitcast(I32)
+                )
+        nc.sync.dma_start(lists[2][:], offs3)
+        nc.sync.dma_start(out=wb_raw[:].bitcast(I32), in_=wb_words[0].rearrange("p c t -> p (c t)").bitcast(I32))
+        for t in range(PACK):
+            nc.sync.dma_start(out=tz_win[t][:], in_=tz_rows[t])
+
+        u_codes = [keep.tile([P, J], U32, name="u_codes%d" % a, align_bytes=64) for a in range(PASSES)]
+        u_sc = [keep.tile([P, J], U8, name="u_sc%d" % a, align_bytes=64) for a in range(PASSES)]
+        u_bf = [keep.tile([P, J, PACK], BF16, name="u_bf%d" % a, align_bytes=64) for a in range(PASSES)]
+        x_g = [keep.tile([P, PACK, J], F32, name="x_g%d" % a) for a in range(PASSES)]
+        x_s = [keep.tile([P, PACK, J], F32, name="x_s%d" % a) for a in range(PASSES)]
+        sums = [keep.tile([P, PACK, B], F32, name="sums%d" % a) for a in range(PASSES)]
+        shift = [keep.tile([P, PACK, B], F32, name="shift%d" % a) for a in range(PASSES)]
+        mean_factor = keep.tile([P, PASSES, PACK], F32, name="mean_factor")
+        nc.scalar.activation(mean_factor[:], fk_sb[:], COPY, scale=-1.0 / GROUP)
+
+        def pick_x(a, t):
+            nc.scalar.activation(x_g[a][:, t, :], x_win[a * PACK + t][:].indirect(lists[0][:]), COPY)
+            nc.vector.tensor_reduce(
+                out=sums[a][:, t, :], in_=x_g[a][:, t, :].rearrange("p (b e) -> p b e", e=GROUP), axis=AX.X, op=ALU.add
+            )
+            nc.gpsimd.tensor_scalar(
+                out=x_s[a][:, t, :],
+                in0=x_g[a][:, t, :],
+                scalar1=fk_sb[:, a, t : t + 1],
+                scalar2=0.0,
+                op0=ALU.mult,
+                op1=ALU.add,
+            )
+
+        def make_shift(a):
+            nc.vector.tensor_tensor(
+                out=shift[a][:],
+                in0=sums[a][:],
+                in1=mean_factor[:, a, :].unsqueeze(2).to_broadcast([P, PACK, B]),
+                op=ALU.mult,
+            )
+
+        def centre(a, cols):
+            groups = slice(cols.start // GROUP, cols.stop // GROUP)
+            count = groups.stop - groups.start
+            nc.vector.tensor_tensor(
+                out=u_bf[a][:, cols, :].rearrange("p (b e) t -> p b t e", e=GROUP),
+                in0=x_s[a][:, :, cols].rearrange("p t (b e) -> p b t e", e=GROUP),
+                in1=shift[a][:, :, groups].rearrange("p t b -> p b t").unsqueeze(3).to_broadcast([P, count, PACK, GROUP]),
+                op=ALU.add,
+            )
+
+        def quantise_u(a, cols):
+            nc.vector.quantize_mx(
+                out=u_codes[a][:, cols].bitcast(E4M3X4),
+                scales=u_sc[a][:, cols],
+                in_=u_bf[a][:, cols, :].rearrange("p j t -> p (j t)"),
+            )
+
+        def deal(out, in_):
+            nc.vector.tensor_copy(out=out.rearrange("p t m -> p m t"), in_=in_.rearrange("p (m t) -> p m t", t=PACK))
+
+        chunk_cols = [slice(c * CHUNK, (c + 1) * CHUNK) for c in range(CHUNKS)]
+
+        for t in range(PACK):
+            pick_x(0, t)
+        nc.vector.tensor_copy(
+            out=w_sc[:].rearrange("p a t m -> p a m t"), in_=ws_raw[:].rearrange("p a (m t) -> p a m t", t=PACK)
+        )
+        deal(wb_sc[:], wbs_raw[:])
+        make_shift(0)
+        pick_x(1, 0)
+        centre(0, slice(0, J))
+        pick_x(1, 1)
+        quantise_u(0, slice(0, J))
+        for t in range(2, PACK):
+            pick_x(1, t)
+        make_shift(1)
+        deal(w_codes[0][:].bitcast(I32), w_raw[0][:].bitcast(I32))
+        centre(1, chunk_cols[0])
+        deal(w_codes[1][:].bitcast(I32), w_raw[1][:].bitcast(I32))
+        for c in range(CHUNKS):
+            quantise_u(1, chunk_cols[c])
+            if c + 1 < CHUNKS:
+                centre(1, chunk_cols[c + 1])
+
+        tb_g = keep.tile([P, PACK, J], F32, name="tb_g")
+        for t in range(PACK):
+            nc.scalar.activation(tb_g[:, t, :], tb_win[t][:].indirect(lists[1][:]), COPY)
+        deal(wb_codes[:].bitcast(I32), wb_raw[:].bitcast(I32))
+        tz_g = keep.tile([P, PACK, J], F32, name="tz_g")
+        for t in range(PACK):
+            nc.scalar.activation(tz_g[:, t, :], tz_win[t][:].indirect(lists[2][:]), COPY)
+
+        a_bank = [psum.tile([P, PACK, CHUNK], F32, name="a_bank%d" % c) for c in range(CHUNKS)]
+        p_bank = [psum.tile([P, PACK, CHUNK], F32, name="p_bank%d" % c) for c in range(CHUNKS)]
+        for a in range(PASSES):
+            for c, cols in enumerate(chunk_cols):
+                for t in range(PACK):
+                    nc.tensor.matmul_mx(
+                        out=a_bank[c][:, t, :],
+                        lhsT=w_codes[a][:, t, :].bitcast(E5M2X4),
+                        lhsT_scale=w_sc[:, a, t, :],
+                        rhs=u_codes[a][:, cols].bitcast(E4M3X4),
+                        rhs_scale=u_sc[a][:, cols],
+                        start=(a == 0 and t == 0),
+                        stop=(a == PASSES - 1 and t == PACK - 1),
+                    )
+
+        h_bf = keep.tile([P, J, PACK], BF16, name="h_bf", align_bytes=64)
+        h_codes = keep.tile([P, J], U32, name="h_codes", align_bytes=64)
+        h_sc = keep.tile([P, J], U8, name="h_sc", align_bytes=64)
+        for c, cols in enumerate(chunk_cols):
+            nc.vector.scalar_tensor_tensor(
+                out=h_bf[:, cols, :],
+                in0=a_bank[c][:].rearrange("p t j -> p j t"),
+                scalar=0.0,
+                in1=tb_g[:, :, cols].rearrange("p t j -> p j t"),
+                op0=ALU.max,
+                op1=ALU.mult,
+            )
+        for c, cols in enumerate(chunk_cols):
+            nc.vector.quantize_mx(
+                out=h_codes[:, cols].bitcast(E4M3X4),
+                scales=h_sc[:, cols],
+                in_=h_bf[:, cols, :].rearrange("p j t -> p (j t)"),
+            )
+            for t in range(PACK):
+                nc.tensor.matmul_mx(
+                    out=p_bank[c][:, t, :],
+                    lhsT=wb_codes[:, t, :].bitcast(E5M2X4),
+                    lhsT_scale=wb_sc[:, t, :],
+                    rhs=h_codes[:, cols].bitcast(E4M3X4),
+                    rhs_scale=h_sc[:, cols],
+                    start=True,
+                    stop=True,
+                )
+
+        y_bf = keep.tile([P, J, PACK], BF16, name="y_bf", align_bytes=64)
+        y_codes = keep.tile([P, J], U32, name="y_codes", align_bytes=64)
+        y_sc = keep.tile([P, J], U8, name="y_sc", align_bytes=64)
+        y_rows = out_0.rearrange("(p t) j -> p t j", t=PACK)
+        y_f32 = [keep.tile([P, PACK, CHUNK], F32, name="y_f32%d" % c) for c in range(CHUNKS)]
+        for c, cols in enumerate(chunk_cols):
+            nc.vector.tensor_tensor(out=y_f32[c][:], in0=p_bank[c][:], in1=tz_g[:, :, cols], op=ALU.mult)
+            nc.sync.dma_start(out=y_rows[:, :, cols], in_=y_f32[c][:])
+            nc.scalar.copy(
+                out=y_bf[:, cols, :].rearrange("p (c i) t -> p c t i", i=4),
+                in_=y_f32[c][:].rearrange("p t (c i) -> p c t i", i=4),
+            )
+        for c, cols in enumerate(chunk_cols):
+            nc.vector.quantize_mx(
+                out=y_codes[:, cols].bitcast(E4M3X4),
+                scales=y_sc[:, cols],
+                in_=y_bf[:, cols, :].rearrange("p j t -> p (j t)"),
+            )
+        nc.sync.dma_start(out=out_1[0].rearrange("p c t -> p (c t)").bitcast(I32), in_=y_codes[:].bitcast(I32))
+        for q in range(4):
+            queue = nc.scalar if q % 2 == 0 else nc.sync
+            queue.dma_start(
+                out=out_2[0, 4 * q : 4 * q + 4, :].bitcast(I32), in_=y_sc[32 * q : 32 * q + 4, :].bitcast(I32)
+            )

@@ -45,8 +45,6 @@ def tile_list_centredpicks_timestable_timeslook_pl_kernel(
         wbs_raw = keep.tile([P, N], U8, name="wbs_raw")
         w_codes = [keep.tile([P, PACK, P], U32, name="w_codes%d" % a, align_bytes=64) for a in range(PASSES)]
         wb_codes = keep.tile([P, PACK, P], U32, name="wb_codes", align_bytes=64)
-        w_sc = keep.tile([P, PASSES, PACK, P], U8, name="w_sc", align_bytes=64)
-        wb_sc = keep.tile([P, PACK, P], U8, name="wb_sc", align_bytes=64)
 
         nc.gpsimd.memset(ws_raw[:].rearrange("p a c -> p (a c)").bitcast(I32), 0)
         nc.gpsimd.memset(wbs_raw[:].bitcast(I32), 0)
@@ -71,71 +69,69 @@ def tile_list_centredpicks_timestable_timeslook_pl_kernel(
 
         nc.scalar.dma_start(out=fk_sb[:], in_=fk.rearrange("(a p t) o -> p a (t o)", a=PASSES, t=PACK))
         nc.sync.dma_start(lists[0][:], offs)
-        load_x(0)
-        load_x(1)
-        for q in (0, 2):
-            load_w_scales(q)
-            load_w_scales(q + 1)
-            load_x(2 + q // 2)
-        for q in (0, 2):
-            load_wb_scales(q)
-            load_wb_scales(q + 1)
-            load_x(4 + q // 2)
-        load_x(6)
+        for i in range(PASSES * PACK):
+            load_x(i)
+            if 2 <= i < 6:
+                load_w_scales(i - 2)
+        for a in range(PASSES):
+            nc.sync.dma_start(out=w_raw[a][:].bitcast(I32), in_=w_words[a].rearrange("p c t -> p (c t)").bitcast(I32))
         nc.sync.dma_start(lists[1][:], offs2)
-        load_x(7)
         for t in range(PACK):
             nc.sync.dma_start(out=tb_win[t][:], in_=tb_rows[t])
-            if t < PASSES:
-                nc.sync.dma_start(
-                    out=w_raw[t][:].bitcast(I32), in_=w_words[t].rearrange("p c t -> p (c t)").bitcast(I32)
-                )
-        nc.sync.dma_start(lists[2][:], offs3)
+            load_wb_scales(t)
         nc.sync.dma_start(out=wb_raw[:].bitcast(I32), in_=wb_words[0].rearrange("p c t -> p (c t)").bitcast(I32))
+        nc.sync.dma_start(lists[2][:], offs3)
         for t in range(PACK):
             nc.sync.dma_start(out=tz_win[t][:], in_=tz_rows[t])
 
         u_codes = [keep.tile([P, J], U32, name="u_codes%d" % a, align_bytes=64) for a in range(PASSES)]
         u_sc = [keep.tile([P, J], U8, name="u_sc%d" % a, align_bytes=64) for a in range(PASSES)]
         u_bf = [keep.tile([P, J, PACK], BF16, name="u_bf%d" % a, align_bytes=64) for a in range(PASSES)]
-        x_g = [keep.tile([P, PACK, J], F32, name="x_g%d" % a) for a in range(PASSES)]
-        x_s = [keep.tile([P, PACK, J], F32, name="x_s%d" % a) for a in range(PASSES)]
-        sums = [keep.tile([P, PACK, B], F32, name="sums%d" % a) for a in range(PASSES)]
-        shift = [keep.tile([P, PACK, B], F32, name="shift%d" % a) for a in range(PASSES)]
-        mean_factor = keep.tile([P, PASSES, PACK], F32, name="mean_factor")
-        nc.scalar.activation(mean_factor[:], fk_sb[:], COPY, scale=-1.0 / GROUP)
+        u_f32 = [keep.tile([P, PACK, J], F32, name="u_f32%d" % a, tag="u_f32%d" % a, align_bytes=64) for a in range(PASSES)]
+        x_g = [keep.tile([P, J], F32, name="x_g%d" % i, tag="x_g%d" % i, align_bytes=64) for i in range(PASSES * PACK)]
+        sums = keep.tile([P, PASSES * PACK, B], F32, name="sums")
+        shift = keep.tile([P, PASSES * PACK, B], F32, name="shift")
+        mean_factor = keep.tile([P, PASSES * PACK], F32, name="mean_factor")
+        factor = fk_sb[:].rearrange("p a t -> p (a t)")
+        nc.scalar.activation(mean_factor[:], factor, COPY, scale=-1.0 / GROUP)
 
-        def pick_x(a, t):
-            nc.scalar.activation(x_g[a][:, t, :], x_win[a * PACK + t][:].indirect(lists[0][:]), COPY)
+        def pick_x(i):
+            if i == 0:
+                half = J // 2
+                nc.scalar.activation(x_g[i][:, :half], x_win[i][:].indirect(lists[0][:, : half // 16]), COPY)
+                nc.vector.tensor_copy(x_g[i][:, half:], x_win[i][:].indirect(lists[0][:, half // 16 :]))
+            else:
+                nc.scalar.activation(x_g[i][:], x_win[i][:].indirect(lists[0][:]), COPY)
             nc.vector.tensor_reduce(
-                out=sums[a][:, t, :], in_=x_g[a][:, t, :].rearrange("p (b e) -> p b e", e=GROUP), axis=AX.X, op=ALU.add
-            )
-            nc.gpsimd.tensor_scalar(
-                out=x_s[a][:, t, :],
-                in0=x_g[a][:, t, :],
-                scalar1=fk_sb[:, a, t : t + 1],
-                scalar2=0.0,
-                op0=ALU.mult,
-                op1=ALU.add,
+                out=sums[:, i, :], in_=x_g[i][:].rearrange("p (b e) -> p b e", e=GROUP), axis=AX.X, op=ALU.add
             )
 
-        def make_shift(a):
+        def centre(first, count):
+            planes = slice(first, first + count)
             nc.vector.tensor_tensor(
-                out=shift[a][:],
-                in0=sums[a][:],
-                in1=mean_factor[:, a, :].unsqueeze(2).to_broadcast([P, PACK, B]),
+                out=shift[:, planes, :],
+                in0=sums[:, planes, :],
+                in1=mean_factor[:, planes].unsqueeze(2).to_broadcast([P, count, B]),
                 op=ALU.mult,
             )
+            for i in range(first, first + count):
+                nc.vector.scalar_tensor_tensor(
+                    out=u_f32[i // PACK][:, i % PACK, :].rearrange("p (b e) -> p b e", e=GROUP),
+                    in0=x_g[i][:].rearrange("p (b e) -> p b e", e=GROUP),
+                    scalar=factor[:, i : i + 1],
+                    in1=shift[:, i, :].unsqueeze(2).to_broadcast([P, B, GROUP]),
+                    op0=ALU.mult,
+                    op1=ALU.add,
+                )
 
-        def centre(a, cols):
-            groups = slice(cols.start // GROUP, cols.stop // GROUP)
-            count = groups.stop - groups.start
-            nc.vector.tensor_tensor(
-                out=u_bf[a][:, cols, :].rearrange("p (b e) t -> p b t e", e=GROUP),
-                in0=x_s[a][:, :, cols].rearrange("p t (b e) -> p b t e", e=GROUP),
-                in1=shift[a][:, :, groups].rearrange("p t b -> p b t").unsqueeze(3).to_broadcast([P, count, PACK, GROUP]),
-                op=ALU.add,
+        def weave(copy, out, in_):
+            copy(
+                out=out.rearrange("p (c i) t -> p c t i", i=4),
+                in_=in_.rearrange("p t (c i) -> p c t i", i=4),
             )
+
+        def round_u(copy, a, cols):
+            weave(copy, u_bf[a][:, cols, :], u_f32[a][:, :, cols])
 
         def quantise_u(a, cols):
             nc.vector.quantize_mx(
@@ -144,45 +140,67 @@ def tile_list_centredpicks_timestable_timeslook_pl_kernel(
                 in_=u_bf[a][:, cols, :].rearrange("p j t -> p (j t)"),
             )
 
-        def deal(out, in_):
-            nc.vector.tensor_copy(out=out.rearrange("p t m -> p m t"), in_=in_.rearrange("p (m t) -> p m t", t=PACK))
+        def deal(copy, out, in_, run):
+            copy(
+                out=out.rearrange("p t (c i) -> p c t i", i=run),
+                in_=in_.rearrange("p (c i t) -> p c t i", i=run, t=PACK),
+            )
 
         chunk_cols = [slice(c * CHUNK, (c + 1) * CHUNK) for c in range(CHUNKS)]
 
-        for t in range(PACK):
-            pick_x(0, t)
-        nc.vector.tensor_copy(
-            out=w_sc[:].rearrange("p a t m -> p a m t"), in_=ws_raw[:].rearrange("p a (m t) -> p a m t", t=PACK)
-        )
-        deal(wb_sc[:], wbs_raw[:])
-        make_shift(0)
-        pick_x(1, 0)
-        centre(0, slice(0, J))
-        pick_x(1, 1)
+        on_vector, on_scalar = nc.vector.tensor_copy, nc.scalar.copy
+        pick_x(0)
+        centre(0, 1)
+        pick_x(1)
+        centre(1, 1)
+        pick_x(2)
+        pick_x(3)
+        centre(2, 2)
+        pick_x(4)
+        round_u(on_vector, 0, slice(0, J))
+        pick_x(5)
+        centre(4, 2)
         quantise_u(0, slice(0, J))
-        for t in range(2, PACK):
-            pick_x(1, t)
-        make_shift(1)
-        deal(w_codes[0][:].bitcast(I32), w_raw[0][:].bitcast(I32))
-        centre(1, chunk_cols[0])
-        deal(w_codes[1][:].bitcast(I32), w_raw[1][:].bitcast(I32))
+        pick_x(6)
+        w_sc = keep.tile([P, PASSES, PACK, P], U8, name="w_sc", align_bytes=64)
+        nc.vector.tensor_copy(
+            out=w_sc[:].rearrange("p a t (c i) -> p a c t i", i=16),
+            in_=ws_raw[:].rearrange("p a (c i t) -> p a c t i", i=16, t=PACK),
+        )
+        centre(6, 1)
+        pick_x(7)
+        centre(7, 1)
+        deal(on_scalar, w_codes[0][:], w_raw[0][:], 4)
+        deal(on_vector, w_codes[1][:].bitcast(I32), w_raw[1][:].bitcast(I32), 4)
+        round_u(on_vector, 1, chunk_cols[0])
         for c in range(CHUNKS):
-            quantise_u(1, chunk_cols[c])
             if c + 1 < CHUNKS:
-                centre(1, chunk_cols[c + 1])
+                round_u(on_vector, 1, chunk_cols[c + 1])
+            quantise_u(1, chunk_cols[c])
 
         tb_g = keep.tile([P, PACK, J], F32, name="tb_g")
-        for t in range(PACK):
-            nc.scalar.activation(tb_g[:, t, :], tb_win[t][:].indirect(lists[1][:]), COPY)
-        deal(wb_codes[:].bitcast(I32), wb_raw[:].bitcast(I32))
         tz_g = keep.tile([P, PACK, J], F32, name="tz_g")
-        for t in range(PACK):
-            nc.scalar.activation(tz_g[:, t, :], tz_win[t][:].indirect(lists[2][:]), COPY)
+
+        def pick(picked, windows, offsets):
+            for t in range(PACK - 1):
+                nc.scalar.activation(picked[:, t, :], windows[t][:].indirect(offsets[:]), COPY)
+            for cols in chunk_cols:
+                nc.scalar.activation(
+                    picked[:, PACK - 1, cols],
+                    windows[PACK - 1][:].indirect(offsets[:, cols.start // 16 : cols.stop // 16]),
+                    COPY,
+                )
+
+        pick(tb_g, tb_win, lists[1])
+        wb_sc = keep.tile([P, PACK, P], U8, name="wb_sc", align_bytes=64)
+        deal(on_vector, wb_sc[:], wbs_raw[:], 16)
+        deal(on_vector, wb_codes[:].bitcast(I32), wb_raw[:].bitcast(I32), 4)
+        pick(tz_g, tz_win, lists[2])
 
         a_bank = [psum.tile([P, PACK, CHUNK], F32, name="a_bank%d" % c) for c in range(CHUNKS)]
         p_bank = [psum.tile([P, PACK, CHUNK], F32, name="p_bank%d" % c) for c in range(CHUNKS)]
-        for a in range(PASSES):
-            for c, cols in enumerate(chunk_cols):
+        for c, cols in enumerate(chunk_cols):
+            for a in range(PASSES):
                 for t in range(PACK):
                     nc.tensor.matmul_mx(
                         out=a_bank[c][:, t, :],
@@ -197,7 +215,9 @@ def tile_list_centredpicks_timestable_timeslook_pl_kernel(
         h_bf = keep.tile([P, J, PACK], BF16, name="h_bf", align_bytes=64)
         h_codes = keep.tile([P, J], U32, name="h_codes", align_bytes=64)
         h_sc = keep.tile([P, J], U8, name="h_sc", align_bytes=64)
-        for c, cols in enumerate(chunk_cols):
+
+        def hidden(c):
+            cols = chunk_cols[c]
             nc.vector.scalar_tensor_tensor(
                 out=h_bf[:, cols, :],
                 in0=a_bank[c][:].rearrange("p t j -> p j t"),
@@ -206,7 +226,11 @@ def tile_list_centredpicks_timestable_timeslook_pl_kernel(
                 op0=ALU.max,
                 op1=ALU.mult,
             )
+
+        hidden(0)
         for c, cols in enumerate(chunk_cols):
+            if c + 1 < CHUNKS:
+                hidden(c + 1)
             nc.vector.quantize_mx(
                 out=h_codes[:, cols].bitcast(E4M3X4),
                 scales=h_sc[:, cols],
@@ -231,11 +255,11 @@ def tile_list_centredpicks_timestable_timeslook_pl_kernel(
         for c, cols in enumerate(chunk_cols):
             nc.vector.tensor_tensor(out=y_f32[c][:], in0=p_bank[c][:], in1=tz_g[:, :, cols], op=ALU.mult)
             nc.sync.dma_start(out=y_rows[:, :, cols], in_=y_f32[c][:])
-            nc.scalar.copy(
-                out=y_bf[:, cols, :].rearrange("p (c i) t -> p c t i", i=4),
-                in_=y_f32[c][:].rearrange("p t (c i) -> p c t i", i=4),
-            )
+            if c + 1 < CHUNKS:
+                weave(on_scalar, y_bf[:, cols, :], y_f32[c][:])
         for c, cols in enumerate(chunk_cols):
+            if c + 2 == CHUNKS:
+                weave(on_vector, y_bf[:, chunk_cols[c + 1], :], y_f32[c + 1][:])
             nc.vector.quantize_mx(
                 out=y_codes[:, cols].bitcast(E4M3X4),
                 scales=y_sc[:, cols],

@@ -22,6 +22,7 @@ AX = mybir.AxisListType
 P = 128
 PACK = 4
 PASSES = K // (P * PACK)
+SPARE = 256
 CHUNK = 128
 CHUNKS = J // CHUNK
 
@@ -37,9 +38,10 @@ def tile_list_centredpicks_timestable_timeslook_pl_kernel(
         lists = [keep.tile([P, J // 16], U16, name="list%d" % i) for i in range(3)]
         fk_sb = keep.tile([P, PASSES, PACK], F32, name="fk_sb")
         x_win = [keep.tile([P, T], F32, name="x_win%d" % i) for i in range(PASSES * PACK)]
-        tb_win = [keep.tile([P, V], F32, name="tb_win%d" % t) for t in range(PACK)]
-        tz_win = [keep.tile([P, Z], F32, name="tz_win%d" % t) for t in range(PACK)]
-        w_raw = [keep.tile([P, R], U32, name="w_raw%d" % a) for a in range(PASSES)]
+        tb_one = [keep.tile([P, V], F32, name="tb_one%d" % e) for e in range(2)]
+        tb_win = [None, keep.tile([P, 2 * V + SPARE], F32, name="tb_win1")]
+        tz_win = [keep.tile([P, 2 * Z + SPARE], F32, name="tz_win%d" % u) for u in range(2)]
+        w_raw = [keep.tile([P, R], U32, name="w_raw%d" % a, tag="w_raw%d" % a) for a in range(PASSES)]
         wb_raw = keep.tile([P, N], U32, name="wb_raw")
         ws_raw = keep.tile([P, PASSES, R], U8, name="ws_raw")
         wbs_raw = keep.tile([P, N], U8, name="wbs_raw")
@@ -48,10 +50,12 @@ def tile_list_centredpicks_timestable_timeslook_pl_kernel(
 
         nc.gpsimd.memset(ws_raw[:].rearrange("p a c -> p (a c)").bitcast(I32), 0)
         nc.gpsimd.memset(wbs_raw[:].bitcast(I32), 0)
+        for window in tb_win[1:] + tz_win:
+            nc.gpsimd.memset(window[:, 2 * V :], 0.0)
 
         x_rows = xf.rearrange("(a p t) c -> a t p c", a=PASSES, t=PACK)
-        tb_rows = tb.rearrange("(p t) c -> t p c", t=PACK)
-        tz_rows = tz.rearrange("(p t) c -> t p c", t=PACK)
+        tb_rows = tb.rearrange("(p u e) c -> u p (e c)", u=2, e=2)
+        tz_rows = tz.rearrange("(p u e) c -> u p (e c)", u=2, e=2)
 
         def load_w_scales(q):
             nc.sync.dma_start(
@@ -71,67 +75,80 @@ def tile_list_centredpicks_timestable_timeslook_pl_kernel(
         nc.sync.dma_start(lists[0][:], offs)
         for i in range(PASSES * PACK):
             load_x(i)
-            if 2 <= i < 6:
-                load_w_scales(i - 2)
-        for a in range(PASSES):
-            nc.sync.dma_start(out=w_raw[a][:].bitcast(I32), in_=w_words[a].rearrange("p c t -> p (c t)").bitcast(I32))
+            if i < 2:
+                load_w_scales(2 * i)
+                load_w_scales(2 * i + 1)
+            if 3 <= i < 7:
+                load_wb_scales(i - 3)
+
+        def load_words(raw, words):
+            nc.sync.dma_start(out=raw[:].bitcast(I32), in_=words.rearrange("p c t -> p (c t)").bitcast(I32))
+
+        load_words(w_raw[0], w_words[0])
         nc.sync.dma_start(lists[1][:], offs2)
-        for t in range(PACK):
-            nc.sync.dma_start(out=tb_win[t][:], in_=tb_rows[t])
-            load_wb_scales(t)
-        nc.sync.dma_start(out=wb_raw[:].bitcast(I32), in_=wb_words[0].rearrange("p c t -> p (c t)").bitcast(I32))
+        nc.sync.dma_start(out=tb_one[0][:], in_=tb_rows[0][:, :V])
+        load_words(w_raw[1], w_words[1])
+        nc.sync.dma_start(out=tb_one[1][:], in_=tb_rows[0][:, V:])
+        nc.sync.dma_start(out=tb_win[1][:, : 2 * V], in_=tb_rows[1])
+        load_words(wb_raw, wb_words[0])
         nc.sync.dma_start(lists[2][:], offs3)
-        for t in range(PACK):
-            nc.sync.dma_start(out=tz_win[t][:], in_=tz_rows[t])
+        for u in range(2):
+            nc.sync.dma_start(out=tz_win[u][:, : 2 * Z], in_=tz_rows[u])
 
         u_codes = [keep.tile([P, J], U32, name="u_codes%d" % a, align_bytes=64) for a in range(PASSES)]
         u_sc = [keep.tile([P, J], U8, name="u_sc%d" % a, align_bytes=64) for a in range(PASSES)]
         u_bf = [keep.tile([P, J, PACK], BF16, name="u_bf%d" % a, align_bytes=64) for a in range(PASSES)]
-        u_f32 = [keep.tile([P, PACK, J], F32, name="u_f32%d" % a, tag="u_f32%d" % a, align_bytes=64) for a in range(PASSES)]
-        x_g = [keep.tile([P, J], F32, name="x_g%d" % i, tag="x_g%d" % i, align_bytes=64) for i in range(PASSES * PACK)]
-        sums = keep.tile([P, PASSES * PACK, B], F32, name="sums")
-        shift = keep.tile([P, PASSES * PACK, B], F32, name="shift")
-        mean_factor = keep.tile([P, PASSES * PACK], F32, name="mean_factor")
-        factor = fk_sb[:].rearrange("p a t -> p (a t)")
-        nc.scalar.activation(mean_factor[:], factor, COPY, scale=-1.0 / GROUP)
+        x_g = [keep.tile([P, PACK, J], F32, name="x_g%d" % a) for a in range(PASSES)]
+        x_s = [keep.tile([P, PACK, J], F32, name="x_s%d" % a) for a in range(PASSES)]
+        sums = [keep.tile([P, PACK, B], F32, name="sums%d" % a) for a in range(PASSES)]
+        shift = [keep.tile([P, PACK, B], F32, name="shift%d" % a) for a in range(PASSES)]
+        mean_factor = keep.tile([P, PASSES, PACK], F32, name="mean_factor")
+        nc.scalar.activation(mean_factor[:], fk_sb[:], COPY, scale=-1.0 / GROUP)
 
-        def pick_x(i):
-            if i == 0:
+        def pick_x(a, t, total=None):
+            total = sums[a][:, t, :] if total is None else total
+            window = x_win[a * PACK + t]
+            if (a, t) == (0, PACK - 1):
                 half = J // 2
-                nc.scalar.activation(x_g[i][:, :half], x_win[i][:].indirect(lists[0][:, : half // 16]), COPY)
-                nc.vector.tensor_copy(x_g[i][:, half:], x_win[i][:].indirect(lists[0][:, half // 16 :]))
+                nc.scalar.activation(x_g[a][:, t, :half], window[:].indirect(lists[0][:, : half // 16]), COPY)
+                nc.vector.tensor_copy(x_g[a][:, t, half:], window[:].indirect(lists[0][:, half // 16 :]))
             else:
-                nc.scalar.activation(x_g[i][:], x_win[i][:].indirect(lists[0][:]), COPY)
+                nc.scalar.activation(x_g[a][:, t, :], window[:].indirect(lists[0][:]), COPY)
             nc.vector.tensor_reduce(
-                out=sums[:, i, :], in_=x_g[i][:].rearrange("p (b e) -> p b e", e=GROUP), axis=AX.X, op=ALU.add
+                out=total, in_=x_g[a][:, t, :].rearrange("p (b e) -> p b e", e=GROUP), axis=AX.X, op=ALU.add
+            )
+            nc.gpsimd.tensor_scalar(
+                out=x_s[a][:, t, :],
+                in0=x_g[a][:, t, :],
+                scalar1=fk_sb[:, a, t : t + 1],
+                scalar2=0.0,
+                op0=ALU.mult,
+                op1=ALU.add,
             )
 
-        def centre(first, count):
-            planes = slice(first, first + count)
+        def make_shift(a, first, stop):
             nc.vector.tensor_tensor(
-                out=shift[:, planes, :],
-                in0=sums[:, planes, :],
-                in1=mean_factor[:, planes].unsqueeze(2).to_broadcast([P, count, B]),
+                out=shift[a][:, first:stop, :],
+                in0=sums[a][:, first:stop, :],
+                in1=mean_factor[:, a, first:stop].unsqueeze(2).to_broadcast([P, stop - first, B]),
                 op=ALU.mult,
             )
-            for i in range(first, first + count):
-                nc.vector.scalar_tensor_tensor(
-                    out=u_f32[i // PACK][:, i % PACK, :].rearrange("p (b e) -> p b e", e=GROUP),
-                    in0=x_g[i][:].rearrange("p (b e) -> p b e", e=GROUP),
-                    scalar=factor[:, i : i + 1],
-                    in1=shift[:, i, :].unsqueeze(2).to_broadcast([P, B, GROUP]),
-                    op0=ALU.mult,
-                    op1=ALU.add,
-                )
+
+        def centre(a, cols):
+            groups = slice(cols.start // GROUP, cols.stop // GROUP)
+            count = groups.stop - groups.start
+            nc.vector.tensor_tensor(
+                out=u_bf[a][:, cols, :].rearrange("p (b e) t -> p b t e", e=GROUP),
+                in0=x_s[a][:, :, cols].rearrange("p t (b e) -> p b t e", e=GROUP),
+                in1=shift[a][:, :, groups].rearrange("p t b -> p b t").unsqueeze(3).to_broadcast([P, count, PACK, GROUP]),
+                op=ALU.add,
+            )
 
         def weave(copy, out, in_):
             copy(
                 out=out.rearrange("p (c i) t -> p c t i", i=4),
                 in_=in_.rearrange("p t (c i) -> p c t i", i=4),
             )
-
-        def round_u(copy, a, cols):
-            weave(copy, u_bf[a][:, cols, :], u_f32[a][:, :, cols])
 
         def quantise_u(a, cols):
             nc.vector.quantize_mx(
@@ -140,62 +157,64 @@ def tile_list_centredpicks_timestable_timeslook_pl_kernel(
                 in_=u_bf[a][:, cols, :].rearrange("p j t -> p (j t)"),
             )
 
-        def deal(copy, out, in_, run):
-            copy(
-                out=out.rearrange("p t (c i) -> p c t i", i=run),
-                in_=in_.rearrange("p (c i t) -> p c t i", i=run, t=PACK),
-            )
+        def deal(copy, out, in_):
+            copy(out=out.rearrange("p t m -> p m t"), in_=in_.rearrange("p (m t) -> p m t", t=PACK))
 
         chunk_cols = [slice(c * CHUNK, (c + 1) * CHUNK) for c in range(CHUNKS)]
 
         on_vector, on_scalar = nc.vector.tensor_copy, nc.scalar.copy
-        pick_x(0)
-        centre(0, 1)
-        pick_x(1)
-        centre(1, 1)
-        pick_x(2)
-        pick_x(3)
-        centre(2, 2)
-        pick_x(4)
-        round_u(on_vector, 0, slice(0, J))
-        pick_x(5)
-        centre(4, 2)
-        quantise_u(0, slice(0, J))
-        pick_x(6)
+        for t in range(PACK - 1):
+            pick_x(0, t)
         w_sc = keep.tile([P, PASSES, PACK, P], U8, name="w_sc", align_bytes=64)
         nc.vector.tensor_copy(
-            out=w_sc[:].rearrange("p a t (c i) -> p a c t i", i=16),
-            in_=ws_raw[:].rearrange("p a (c i t) -> p a c t i", i=16, t=PACK),
+            out=w_sc[:].rearrange("p a t (c i) -> p c a t i", i=16),
+            in_=ws_raw[:].rearrange("p a (c i t) -> p c a t i", i=16, t=PACK),
         )
-        centre(6, 1)
-        pick_x(7)
-        centre(7, 1)
-        deal(on_scalar, w_codes[0][:], w_raw[0][:], 4)
-        deal(on_vector, w_codes[1][:].bitcast(I32), w_raw[1][:].bitcast(I32), 4)
-        round_u(on_vector, 1, chunk_cols[0])
+        pick_x(0, PACK - 1)
+        make_shift(0, 0, PACK)
+        centre(0, slice(0, J))
+        pick_x(1, 0)
+        pick_x(1, 1)
+        quantise_u(0, slice(0, J))
+        pick_x(1, 2)
+        make_shift(1, 0, PACK - 1)
+        wb_sc = keep.tile([P, PACK, P], U8, name="wb_sc", align_bytes=64)
+        nc.vector.tensor_copy(
+            out=wb_sc[:].rearrange("p t (c i) -> p c t i", i=16),
+            in_=wbs_raw[:].rearrange("p (c i t) -> p c t i", i=16, t=PACK),
+        )
+        deal(on_vector, w_codes[0][:].bitcast(I32), w_raw[0][:].bitcast(I32))
+        last_sums = keep.tile([P, B], F32, name="last_sums", tag="w_raw0")
+        pick_x(1, 3, last_sums[:])
+        nc.vector.tensor_scalar(
+            out=shift[1][:, PACK - 1, :],
+            in0=last_sums[:],
+            scalar1=mean_factor[:, 1, PACK - 1 :],
+            scalar2=None,
+            op0=ALU.mult,
+        )
+        centre(1, chunk_cols[0])
+        deal(on_vector, w_codes[1][:].bitcast(I32), w_raw[1][:].bitcast(I32))
         for c in range(CHUNKS):
             if c + 1 < CHUNKS:
-                round_u(on_vector, 1, chunk_cols[c + 1])
+                centre(1, chunk_cols[c + 1])
             quantise_u(1, chunk_cols[c])
 
-        tb_g = keep.tile([P, PACK, J], F32, name="tb_g")
-        tz_g = keep.tile([P, PACK, J], F32, name="tz_g")
+        tb_g = [keep.tile([P, PACK, CHUNK], F32, name="tb_g%d" % c) for c in range(CHUNKS)]
+        tz_g = [keep.tile([P, PACK, CHUNK], F32, name="tz_g%d" % c) for c in range(CHUNKS)]
+
+        def pair_windows(pair):
+            return [pair[:, e * V : (e + 1) * V + SPARE] for e in range(2)]
 
         def pick(picked, windows, offsets):
-            for t in range(PACK - 1):
-                nc.scalar.activation(picked[:, t, :], windows[t][:].indirect(offsets[:]), COPY)
-            for cols in chunk_cols:
-                nc.scalar.activation(
-                    picked[:, PACK - 1, cols],
-                    windows[PACK - 1][:].indirect(offsets[:, cols.start // 16 : cols.stop // 16]),
-                    COPY,
-                )
+            order = [(t, c) for t in (0, 1) for c in range(CHUNKS)] + [(t, c) for c in range(CHUNKS) for t in (2, 3)]
+            for t, c in order:
+                columns = slice(c * CHUNK // 16, (c + 1) * CHUNK // 16)
+                nc.scalar.activation(picked[c][:, t, :], windows[t].indirect(offsets[:, columns]), COPY)
 
-        pick(tb_g, tb_win, lists[1])
-        wb_sc = keep.tile([P, PACK, P], U8, name="wb_sc", align_bytes=64)
-        deal(on_vector, wb_sc[:], wbs_raw[:], 16)
-        deal(on_vector, wb_codes[:].bitcast(I32), wb_raw[:].bitcast(I32), 4)
-        pick(tz_g, tz_win, lists[2])
+        pick(tb_g, [tb_one[0][:], tb_one[1][:]] + pair_windows(tb_win[1]), lists[1])
+        deal(on_vector, wb_codes[:].bitcast(I32), wb_raw[:].bitcast(I32))
+        pick(tz_g, pair_windows(tz_win[0]) + pair_windows(tz_win[1]), lists[2])
 
         a_bank = [psum.tile([P, PACK, CHUNK], F32, name="a_bank%d" % c) for c in range(CHUNKS)]
         p_bank = [psum.tile([P, PACK, CHUNK], F32, name="p_bank%d" % c) for c in range(CHUNKS)]
@@ -222,7 +241,7 @@ def tile_list_centredpicks_timestable_timeslook_pl_kernel(
                 out=h_bf[:, cols, :],
                 in0=a_bank[c][:].rearrange("p t j -> p j t"),
                 scalar=0.0,
-                in1=tb_g[:, :, cols].rearrange("p t j -> p j t"),
+                in1=tb_g[c][:].rearrange("p t j -> p j t"),
                 op0=ALU.max,
                 op1=ALU.mult,
             )
@@ -251,21 +270,22 @@ def tile_list_centredpicks_timestable_timeslook_pl_kernel(
         y_codes = keep.tile([P, J], U32, name="y_codes", align_bytes=64)
         y_sc = keep.tile([P, J], U8, name="y_sc", align_bytes=64)
         y_rows = out_0.rearrange("(p t) j -> p t j", t=PACK)
+        y_words = out_1[0].rearrange("p c t -> p (c t)").bitcast(I32)
         y_f32 = [keep.tile([P, PACK, CHUNK], F32, name="y_f32%d" % c) for c in range(CHUNKS)]
         for c, cols in enumerate(chunk_cols):
-            nc.vector.tensor_tensor(out=y_f32[c][:], in0=p_bank[c][:], in1=tz_g[:, :, cols], op=ALU.mult)
+            nc.vector.tensor_tensor(out=y_f32[c][:], in0=p_bank[c][:], in1=tz_g[c][:], op=ALU.mult)
             nc.sync.dma_start(out=y_rows[:, :, cols], in_=y_f32[c][:])
             if c + 1 < CHUNKS:
                 weave(on_scalar, y_bf[:, cols, :], y_f32[c][:])
-        for c, cols in enumerate(chunk_cols):
-            if c + 2 == CHUNKS:
-                weave(on_vector, y_bf[:, chunk_cols[c + 1], :], y_f32[c + 1][:])
+        last = chunk_cols[-1]
+        weave(on_vector, y_bf[:, last, :], y_f32[-1][:])
+        for cols in (slice(0, last.start), last):
             nc.vector.quantize_mx(
                 out=y_codes[:, cols].bitcast(E4M3X4),
                 scales=y_sc[:, cols],
                 in_=y_bf[:, cols, :].rearrange("p j t -> p (j t)"),
             )
-        nc.sync.dma_start(out=out_1[0].rearrange("p c t -> p (c t)").bitcast(I32), in_=y_codes[:].bitcast(I32))
+            nc.sync.dma_start(out=y_words[:, cols], in_=y_codes[:, cols].bitcast(I32))
         for q in range(4):
             queue = nc.scalar if q % 2 == 0 else nc.sync
             queue.dma_start(

from contextlib import ExitStack

import concourse.mybir as mybir

K, T, J, R, V, N, Z = 1024, 1024, 384, 512, 512, 512, 512
GROUP = 8
B = J // GROUP
FLOPS = 2 * K * R * J + 2 * R * N * J

F32 = mybir.dt.float32
BF16 = mybir.dt.bfloat16
I32 = mybir.dt.int32
U32 = mybir.dt.uint32
U16 = mybir.dt.uint16
U8 = mybir.dt.uint8
E4M3X4 = mybir.dt.float8_e4m3fn_x4
E5M2X4 = mybir.dt.float8_e5m2_x4
ALU = mybir.AluOpType
COPY = mybir.ActivationFunctionType.Copy
AX = mybir.AxisListType

P = 128
PACK = 4
PASSES = K // (P * PACK)
SPARE = 256
CHUNK = 128
CHUNKS = J // CHUNK


def tile_list_centredpicks_timestable_timeslook_pl_kernel(
    tc, xf, fk, w_words, w_scales, tb, wb_words, wb_scales, tz, offs, offs2, offs3, out_0, out_1, out_2
):
    nc = tc.nc
    with ExitStack() as ctx:
        keep = ctx.enter_context(tc.tile_pool(name="keep", bufs=1))
        psum = ctx.enter_context(tc.psum_pool(name="psum", bufs=1))

        lists = [keep.tile([P, J // 16], U16, name="list%d" % i) for i in range(3)]
        fk_sb = keep.tile([P, PASSES, PACK], F32, name="fk_sb")
        x_win = [keep.tile([P, T], F32, name="x_win%d" % i) for i in range(PASSES * PACK)]
        tb_one = [keep.tile([P, V], F32, name="tb_one%d" % e) for e in range(2)]
        tb_win = [None, keep.tile([P, 2 * V + SPARE], F32, name="tb_win1")]
        tz_win = [keep.tile([P, 2 * Z + SPARE], F32, name="tz_win%d" % u) for u in range(2)]
        w_raw = [keep.tile([P, R], U32, name="w_raw%d" % a, tag="w_raw%d" % a) for a in range(PASSES)]
        wb_raw = keep.tile([P, N], U32, name="wb_raw")
        ws_raw = keep.tile([P, PASSES, R], U8, name="ws_raw")
        wbs_raw = keep.tile([P, N], U8, name="wbs_raw")
        w_codes = [keep.tile([P, PACK, P], U32, name="w_codes%d" % a, align_bytes=64) for a in range(PASSES)]
        wb_codes = keep.tile([P, PACK, P], U32, name="wb_codes", align_bytes=64)

        nc.gpsimd.memset(ws_raw[:].rearrange("p a c -> p (a c)").bitcast(I32), 0)
        nc.gpsimd.memset(wbs_raw[:].bitcast(I32), 0)
        for window in tb_win[1:] + tz_win:
            nc.gpsimd.memset(window[:, 2 * V :], 0.0)

        x_rows = xf.rearrange("(a p t) c -> a t p c", a=PASSES, t=PACK)
        tb_rows = tb.rearrange("(p u e) c -> u p (e c)", u=2, e=2)
        tz_rows = tz.rearrange("(p u e) c -> u p (e c)", u=2, e=2)

        def load_w_scales(q):
            nc.sync.dma_start(
                out=ws_raw[32 * q : 32 * q + 4].bitcast(I32),
                in_=w_scales[:, 4 * q : 4 * q + 4, :].rearrange("a r c -> r a c").bitcast(I32),
            )

        def load_wb_scales(q):
            nc.sync.dma_start(
                out=wbs_raw[32 * q : 32 * q + 4].bitcast(I32), in_=wb_scales[0, 4 * q : 4 * q + 4, :].bitcast(I32)
            )

        def load_x(i):
            nc.sync.dma_start(out=x_win[i][:], in_=x_rows[i // PACK, i % PACK])

        nc.scalar.dma_start(out=fk_sb[:], in_=fk.rearrange("(a p t) o -> p a (t o)", a=PASSES, t=PACK))
        nc.sync.dma_start(lists[0][:], offs)
        for i in range(PASSES * PACK):
            load_x(i)
            if i < 2:
                load_w_scales(2 * i)
                load_w_scales(2 * i + 1)
            if 3 <= i < 7:
                load_wb_scales(i - 3)

        def load_words(raw, words):
            nc.sync.dma_start(out=raw[:].bitcast(I32), in_=words.rearrange("p c t -> p (c t)").bitcast(I32))

        load_words(w_raw[0], w_words[0])
        nc.sync.dma_start(lists[1][:], offs2)
        nc.sync.dma_start(out=tb_one[0][:], in_=tb_rows[0][:, :V])
        load_words(w_raw[1], w_words[1])
        nc.sync.dma_start(out=tb_one[1][:], in_=tb_rows[0][:, V:])
        nc.sync.dma_start(out=tb_win[1][:, : 2 * V], in_=tb_rows[1])
        load_words(wb_raw, wb_words[0])
        nc.sync.dma_start(lists[2][:], offs3)
        for u in range(2):
            nc.sync.dma_start(out=tz_win[u][:, : 2 * Z], in_=tz_rows[u])

        u_codes = [keep.tile([P, J], U32, name="u_codes%d" % a, align_bytes=64) for a in range(PASSES)]
        u_sc = [keep.tile([P, J], U8, name="u_sc%d" % a, align_bytes=64) for a in range(PASSES)]
        u_bf = [keep.tile([P, J, PACK], BF16, name="u_bf%d" % a, align_bytes=64) for a in range(PASSES)]
        x_g = [keep.tile([P, PACK, J], F32, name="x_g%d" % a) for a in range(PASSES)]
        x_s = [keep.tile([P, PACK, J], F32, name="x_s%d" % a) for a in range(PASSES)]
        sums = [keep.tile([P, PACK, B], F32, name="sums%d" % a) for a in range(PASSES)]
        shift = [keep.tile([P, PACK, B], F32, name="shift%d" % a) for a in range(PASSES)]
        mean_factor = keep.tile([P, PASSES, PACK], F32, name="mean_factor")
        nc.scalar.activation(mean_factor[:], fk_sb[:], COPY, scale=-1.0 / GROUP)

        def pick_x(a, t, total=None):
            total = sums[a][:, t, :] if total is None else total
            window = x_win[a * PACK + t]
            if (a, t) == (0, PACK - 1):
                half = J // 2
                nc.scalar.activation(x_g[a][:, t, :half], window[:].indirect(lists[0][:, : half // 16]), COPY)
                nc.vector.tensor_copy(x_g[a][:, t, half:], window[:].indirect(lists[0][:, half // 16 :]))
            else:
                nc.scalar.activation(x_g[a][:, t, :], window[:].indirect(lists[0][:]), COPY)
            nc.vector.tensor_reduce(
                out=total, in_=x_g[a][:, t, :].rearrange("p (b e) -> p b e", e=GROUP), axis=AX.X, op=ALU.add
            )
            nc.gpsimd.tensor_scalar(
                out=x_s[a][:, t, :],
                in0=x_g[a][:, t, :],
                scalar1=fk_sb[:, a, t : t + 1],
                scalar2=0.0,
                op0=ALU.mult,
                op1=ALU.add,
            )

        def make_shift(a, first, stop):
            nc.vector.tensor_tensor(
                out=shift[a][:, first:stop, :],
                in0=sums[a][:, first:stop, :],
                in1=mean_factor[:, a, first:stop].unsqueeze(2).to_broadcast([P, stop - first, B]),
                op=ALU.mult,
            )

        def centre(a, cols):
            groups = slice(cols.start // GROUP, cols.stop // GROUP)
            count = groups.stop - groups.start
            nc.vector.tensor_tensor(
                out=u_bf[a][:, cols, :].rearrange("p (b e) t -> p b t e", e=GROUP),
                in0=x_s[a][:, :, cols].rearrange("p t (b e) -> p b t e", e=GROUP),
                in1=shift[a][:, :, groups].rearrange("p t b -> p b t").unsqueeze(3).to_broadcast([P, count, PACK, GROUP]),
                op=ALU.add,
            )

        def weave(copy, out, in_):
            copy(
                out=out.rearrange("p (c i) t -> p c t i", i=4),
                in_=in_.rearrange("p t (c i) -> p c t i", i=4),
            )

        def quantise_u(a, cols):
            nc.vector.quantize_mx(
                out=u_codes[a][:, cols].bitcast(E4M3X4),
                scales=u_sc[a][:, cols],
                in_=u_bf[a][:, cols, :].rearrange("p j t -> p (j t)"),
            )

        def deal(copy, out, in_):
            copy(out=out.rearrange("p t m -> p m t"), in_=in_.rearrange("p (m t) -> p m t", t=PACK))

        chunk_cols = [slice(c * CHUNK, (c + 1) * CHUNK) for c in range(CHUNKS)]

        on_vector, on_scalar = nc.vector.tensor_copy, nc.scalar.copy
        for t in range(PACK - 1):
            pick_x(0, t)
        w_sc = keep.tile([P, PASSES, PACK, P], U8, name="w_sc", align_bytes=64)
        nc.vector.tensor_copy(
            out=w_sc[:].rearrange("p a t (c i) -> p c a t i", i=16),
            in_=ws_raw[:].rearrange("p a (c i t) -> p c a t i", i=16, t=PACK),
        )
        pick_x(0, PACK - 1)
        make_shift(0, 0, PACK)
        centre(0, slice(0, J))
        pick_x(1, 0)
        pick_x(1, 1)
        quantise_u(0, slice(0, J))
        pick_x(1, 2)
        make_shift(1, 0, PACK - 1)
        wb_sc = keep.tile([P, PACK, P], U8, name="wb_sc", align_bytes=64)
        nc.vector.tensor_copy(
            out=wb_sc[:].rearrange("p t (c i) -> p c t i", i=16),
            in_=wbs_raw[:].rearrange("p (c i t) -> p c t i", i=16, t=PACK),
        )
        deal(on_vector, w_codes[0][:].bitcast(I32), w_raw[0][:].bitcast(I32))
        last_sums = keep.tile([P, B], F32, name="last_sums", tag="w_raw0")
        pick_x(1, 3, last_sums[:])
        nc.vector.tensor_scalar(
            out=shift[1][:, PACK - 1, :],
            in0=last_sums[:],
            scalar1=mean_factor[:, 1, PACK - 1 :],
            scalar2=None,
            op0=ALU.mult,
        )
        centre(1, chunk_cols[0])
        deal(on_vector, w_codes[1][:].bitcast(I32), w_raw[1][:].bitcast(I32))
        for c in range(CHUNKS):
            if c + 1 < CHUNKS:
                centre(1, chunk_cols[c + 1])
            quantise_u(1, chunk_cols[c])

        tb_g = [keep.tile([P, PACK, CHUNK], F32, name="tb_g%d" % c) for c in range(CHUNKS)]
        tz_g = [keep.tile([P, PACK, CHUNK], F32, name="tz_g%d" % c) for c in range(CHUNKS)]

        def pair_windows(pair):
            return [pair[:, e * V : (e + 1) * V + SPARE] for e in range(2)]

        def pick(picked, windows, offsets):
            order = [(t, c) for t in (0, 1) for c in range(CHUNKS)] + [(t, c) for c in range(CHUNKS) for t in (2, 3)]
            for t, c in order:
                columns = slice(c * CHUNK // 16, (c + 1) * CHUNK // 16)
                nc.scalar.activation(picked[c][:, t, :], windows[t].indirect(offsets[:, columns]), COPY)

        pick(tb_g, [tb_one[0][:], tb_one[1][:]] + pair_windows(tb_win[1]), lists[1])
        deal(on_vector, wb_codes[:].bitcast(I32), wb_raw[:].bitcast(I32))
        pick(tz_g, pair_windows(tz_win[0]) + pair_windows(tz_win[1]), lists[2])

        a_bank = [psum.tile([P, PACK, CHUNK], F32, name="a_bank%d" % c) for c in range(CHUNKS)]
        p_bank = [psum.tile([P, PACK, CHUNK], F32, name="p_bank%d" % c) for c in range(CHUNKS)]
        for c, cols in enumerate(chunk_cols):
            for a in range(PASSES):
                for t in range(PACK):
                    nc.tensor.matmul_mx(
                        out=a_bank[c][:, t, :],
                        lhsT=w_codes[a][:, t, :].bitcast(E5M2X4),
                        lhsT_scale=w_sc[:, a, t, :],
                        rhs=u_codes[a][:, cols].bitcast(E4M3X4),
                        rhs_scale=u_sc[a][:, cols],
                        start=(a == 0 and t == 0),
                        stop=(a == PASSES - 1 and t == PACK - 1),
                    )

        h_bf = keep.tile([P, J, PACK], BF16, name="h_bf", align_bytes=64)
        h_codes = keep.tile([P, J], U32, name="h_codes", align_bytes=64)
        h_sc = keep.tile([P, J], U8, name="h_sc", align_bytes=64)

        def hidden(c):
            cols = chunk_cols[c]
            nc.vector.scalar_tensor_tensor(
                out=h_bf[:, cols, :],
                in0=a_bank[c][:].rearrange("p t j -> p j t"),
                scalar=0.0,
                in1=tb_g[c][:].rearrange("p t j -> p j t"),
                op0=ALU.max,
                op1=ALU.mult,
            )

        hidden(0)
        for c, cols in enumerate(chunk_cols):
            if c + 1 < CHUNKS:
                hidden(c + 1)
            nc.vector.quantize_mx(
                out=h_codes[:, cols].bitcast(E4M3X4),
                scales=h_sc[:, cols],
                in_=h_bf[:, cols, :].rearrange("p j t -> p (j t)"),
            )
            for t in range(PACK):
                nc.tensor.matmul_mx(
                    out=p_bank[c][:, t, :],
                    lhsT=wb_codes[:, t, :].bitcast(E5M2X4),
                    lhsT_scale=wb_sc[:, t, :],
                    rhs=h_codes[:, cols].bitcast(E4M3X4),
                    rhs_scale=h_sc[:, cols],
                    start=True,
                    stop=True,
                )

        y_bf = keep.tile([P, J, PACK], BF16, name="y_bf", align_bytes=64)
        y_codes = keep.tile([P, J], U32, name="y_codes", align_bytes=64)
        y_sc = keep.tile([P, J], U8, name="y_sc", align_bytes=64)
        y_rows = out_0.rearrange("(p t) j -> p t j", t=PACK)
        y_words = out_1[0].rearrange("p c t -> p (c t)").bitcast(I32)
        y_f32 = [keep.tile([P, PACK, CHUNK], F32, name="y_f32%d" % c) for c in range(CHUNKS)]
        for c, cols in enumerate(chunk_cols):
            nc.vector.tensor_tensor(out=y_f32[c][:], in0=p_bank[c][:], in1=tz_g[c][:], op=ALU.mult)
            nc.sync.dma_start(out=y_rows[:, :, cols], in_=y_f32[c][:])
            if c + 1 < CHUNKS:
                weave(on_scalar, y_bf[:, cols, :], y_f32[c][:])
        last = chunk_cols[-1]
        weave(on_vector, y_bf[:, last, :], y_f32[-1][:])
        for cols in (slice(0, last.start), last):
            nc.vector.quantize_mx(
                out=y_codes[:, cols].bitcast(E4M3X4),
                scales=y_sc[:, cols],
                in_=y_bf[:, cols, :].rearrange("p j t -> p (j t)"),
            )
            nc.sync.dma_start(out=y_words[:, cols], in_=y_codes[:, cols].bitcast(I32))
        for q in range(4):
            queue = nc.scalar if q % 2 == 0 else nc.sync
            queue.dma_start(
                out=out_2[0, 4 * q : 4 * q + 4, :].bitcast(I32), in_=y_sc[32 * q : 32 * q + 4, :].bitcast(I32)
            )
